import numpy as np
import ml_dtypes


def mxq(x, axis, fmt="e4m3"):
    dtype, down = {"e4m3": (ml_dtypes.float8_e4m3fn, 7), "e5m2": (ml_dtypes.float8_e5m2, 14)}[fmt]
    v = np.moveaxis(np.asarray(x, np.float32).astype(ml_dtypes.bfloat16).astype(np.float64), axis, -1)
    blocks = v.reshape(v.shape[:-1] + (-1, 32))
    amax = np.abs(blocks).max(-1, keepdims=True)
    byte = np.maximum(np.where(amax > 0, np.frexp(amax)[1] - 1 + 127, 0) - down, 1)
    scale = np.exp2(byte - 127.0)
    codes = (blocks / scale).astype(np.float32).astype(dtype).astype(np.float64)
    return np.moveaxis((codes * scale).reshape(v.shape), -1, axis)


WIDE = False


def mx_kscale(k):
    if not WIDE:
        return np.ones(k)
    levels = np.array([10, -10, 5, -5, 0])
    if k % 512:
        return np.exp2(np.random.permutation(np.resize(levels, k // 32))).repeat(32)
    a = np.empty((k // 512, 16))
    for p in range(k // 512):
        a[p, :8] = np.random.permutation(np.resize(levels, 8))
        for g in range(8):
            far = levels[np.abs(levels - a[p, g]) >= 10]
            a[p, g + 8] = far[np.random.randint(len(far))]
    return np.exp2(a.ravel()).repeat(32)


BF16 = ml_dtypes.bfloat16


def bf(x):
    return np.asarray(x, np.float32).astype(BF16)


def f64(x):
    return np.asarray(x).astype(np.float64)


V, B, D, H, O = 2, 512, 512, 512, 512
C = 2 * H


def sigmoid(v):
    return 1.0 / (1.0 + np.exp(-v))


def project(xi, weight, bias):
    return sigmoid((xi @ weight) + bias) - 0.5


def draw0():
    s, t = mx_kscale(D), mx_kscale(C)
    return {"x": bf(np.random.standard_normal((V, B, D)) * s),
            "p": bf(np.random.standard_normal((V, D, H)) / np.sqrt(D) / s[:, None]),
            "b": bf(np.random.standard_normal((V, H)) * 0.3),
            "g": bf((1.0 + 0.1 * np.random.standard_normal(C)) * t),
            "wd": bf(np.random.standard_normal((C, O)) * 4.0 / np.sqrt(C) / t[:, None]),
            "bd": bf(np.random.standard_normal(O) * 0.3)}


def core(x, p, b, g, wd, bd):
    xq = mxq(f64(x), 2, "e4m3")
    pq = mxq(f64(p), 1, "e4m3")
    bias, gain = f64(b), f64(g)
    m_0 = project(xq[0], pq[0], bias[0])
    m_1 = project(xq[1], pq[0], bias[0])
    s_0 = project(xq[0], pq[1], bias[1])
    s_1 = project(xq[1], pq[1], bias[1])
    c_0 = np.concatenate([m_0, s_0], axis=-1)
    c_1 = np.concatenate([m_1, s_1], axis=-1)
    q = mxq(np.stack([c_0, c_1], axis=0) * gain, 2, "e4m3")
    q_2 = np.concatenate([q[1][:, :H], q[0][:, H:]], axis=-1)
    q_3 = np.concatenate([q[0][:, :H], q[1][:, H:]], axis=-1)
    cq = np.stack([q[0], q[1], q_2, q_3], axis=0)
    return sigmoid((cq @ mxq(f64(wd), 0, "e4m3")) + f64(bd))


def e4m3fn_bytes(y):
    return np.clip(np.asarray(y, np.float64), -448.0, 448.0).astype(np.float32).astype(ml_dtypes.float8_e4m3fn).view(np.uint8)


def e4m3fn_values(b):
    return np.asarray(b, np.uint8).view(ml_dtypes.float8_e4m3fn).astype(np.float64)


def setup_inputs():
    d = draw0()
    x0 = np.asarray(d['x']).astype(np.float64)
    s = (np.max(np.abs(x0), axis=(0, 1), keepdims=True) / 448.0).astype(np.float32)
    out = {}
    for k, v in d.items():
        if k == 'x':
            out['x_bytes'] = e4m3fn_bytes(x0 / s.astype(np.float64))
            out['x_scale'] = s
        else:
            out[k] = v
    return out


def reference(x_bytes, x_scale, p, b, g, wd, bd):
    return core(e4m3fn_values(x_bytes) * x_scale.astype(np.float64), p, b, g, wd, bd)

@@ -1,0 +1,258 @@
+from contextlib import ExitStack
+
+import concourse.mybir as mybir
+from concourse.masks import make_identity
+
+F32 = mybir.dt.float32
+BF16 = mybir.dt.bfloat16
+U32 = mybir.dt.uint32
+U8 = mybir.dt.uint8
+FP8 = mybir.dt.float8_e4m3fn
+FP8X4 = mybir.dt.float8_e4m3fn_x4
+ACT = mybir.ActivationFunctionType
+ALU = mybir.AluOpType
+
+P = 128
+SETS = 2
+TOK = 512
+K1 = 512
+HID = 512
+OUTC = 512
+PACK = 4
+RT = 4
+HALVES = 2
+HN = TOK // HALVES
+
+FLOPS = 2 * 12 * 512 * 512 * 512
+
+
+def tile_switchtabmutualsalientswap_kernel(tc, x_bytes, x_scale, p, b, g, wd, bd, out):
+    nc = tc.nc
+    with ExitStack() as ctx:
+        keep = ctx.enter_context(tc.tile_pool(name="keep", bufs=1))
+        psum = ctx.enter_context(tc.psum_pool(name="psum", bufs=8))
+        ctx.enter_context(tc.manual_schedule())
+
+        def sb(shape, dtype, name):
+            return keep.tile(shape, dtype, name=name, align_bytes=64)
+
+        xb = [sb([P, RT * K1], U8, f"xb{i}") for i in range(SETS)]
+        xw = [sb([P, RT * K1], BF16, f"xw{i}") for i in range(SETS)]
+        xg = [sb([P, TOK * PACK], BF16, f"xg{i}") for i in range(SETS)]
+        xc = [sb([P, TOK], U32, f"xc{i}") for i in range(SETS)]
+        xs = [sb([P, TOK], U8, f"xs{i}") for i in range(SETS)]
+        pr = [sb([P, PACK, HID], BF16, f"pr{v}") for v in range(2)]
+        pg = [sb([P, HID * PACK], BF16, f"pg{v}") for v in range(2)]
+        pc = [sb([P, HID], U32, f"pc{v}") for v in range(2)]
+        psc = [sb([P, HID], U8, f"psc{v}") for v in range(2)]
+        wr = [sb([P, PACK, OUTC], BF16, f"wr{h}") for h in range(2)]
+        wg = [sb([P, OUTC * PACK], BF16, f"wg{h}") for h in range(2)]
+        wc = [sb([P, OUTC], U32, f"wc{h}") for h in range(2)]
+        ws = [sb([P, OUTC], U8, f"ws{h}") for h in range(2)]
+        sc = sb([P, PACK], F32, "sc")
+        b_sb = sb([P, 2 * PACK], BF16, "b_sb")
+        g_sb = sb([P, 2 * PACK], BF16, "g_sb")
+        bh = sb([P, 2 * PACK], F32, "bh")
+        gh = sb([P, 2 * PACK], F32, "gh")
+        bdb = sb([P, OUTC], BF16, "bdb")
+        ident = sb([P, P], F32, "ident")
+        warm = sb([P, 1], F32, "warm")
+        th = [[sb([P, PACK, TOK], F32, f"th{i}{h}") for h in range(2)] for i in range(SETS)]
+        cg = [[[sb([P, HN * PACK], BF16, f"cg{i}{h}{n}") for n in range(HALVES)] for h in range(2)] for i in range(SETS)]
+        cc = [[[sb([P, HN], U32, f"cc{i}{h}{n}") for n in range(HALVES)] for h in range(2)] for i in range(SETS)]
+        cs = [[[sb([P, HN], U8, f"cs{i}{h}{n}") for n in range(HALVES)] for h in range(2)] for i in range(SETS)]
+        zo = [[sb([P, OUTC], F32, f"zo{j}{r}") for r in range(RT)] for j in range(4)]
+
+        def load_x(i, lo, hi):
+            nc.sync.dma_start(
+                out=xb[i][:, lo * K1 : hi * K1],
+                in_=x_bytes[i].rearrange("(p r) k -> p (r k)", r=RT)[:, lo * K1 : hi * K1],
+            )
+
+        def load_p(v):
+            nc.sync.dma_start(out=pr[v][:], in_=p[v].rearrange("(p j) c -> p j c", j=PACK))
+
+        nc.gpsimd.memset(warm[:], 0.0)
+        nc.scalar.activation(out=warm[:], in_=warm[:], func=ACT.Sigmoid)
+        load_x(0, 0, 2)
+        load_x(0, 2, 4)
+        make_identity(nc, ident[:])
+        load_p(0)
+        nc.sync.dma_start(out=sc[:], in_=x_scale.rearrange("a b (p t) -> p (a b t)", t=PACK))
+        nc.sync.dma_start(out=b_sb[:].rearrange("p (v t) -> p v t", t=PACK), in_=b.rearrange("v (p t) -> p v t", t=PACK))
+        load_p(1)
+        load_x(1, 0, 4)
+        nc.sync.dma_start(out=g_sb[:].rearrange("p (h t) -> p h t", t=PACK), in_=g.rearrange("(h p t) -> p h t", t=PACK, h=2))
+        for h in range(2):
+            nc.sync.dma_start(out=wr[h][:], in_=wd[h * HID : (h + 1) * HID, :].rearrange("(p j) o -> p j o", j=PACK))
+        nc.sync.dma_start(out=bdb[:], in_=bd.partition_broadcast(P))
+
+        def cast_x(eng, i, r):
+            cols = slice(r * K1, (r + 1) * K1)
+            if eng == "s":
+                nc.scalar.copy(out=xw[i][:, cols], in_=xb[i][:, cols].bitcast(FP8))
+            else:
+                nc.vector.tensor_copy(out=xw[i][:, cols], in_=xb[i][:, cols].bitcast(FP8))
+
+        xps = {}
+
+        def turn_x(i, pair):
+            words = xw[i][:].bitcast(F32)
+            bank = psum.tile([P, 2 * HN], F32, name="bank")
+            for q in range(2):
+                r = 2 * pair + q
+                for u in range(2):
+                    nc.tensor.transpose(
+                        bank[:, u * HN + q * P : u * HN + (q + 1) * P],
+                        words[:, r * (K1 // 2) + u : (r + 1) * (K1 // 2) : 2],
+                        ident[:],
+                    )
+            xps[i, pair] = bank
+
+        def scale_x(i, pair):
+            nc.vector.tensor_tensor(
+                out=xg[i][:, pair * HN * PACK : (pair + 1) * HN * PACK].rearrange("p (n u e) -> p n u e", u=2, e=2),
+                in0=xps[i, pair][:].bitcast(BF16).rearrange("p (u n e) -> p n u e", u=2, e=2),
+                in1=sc[:].rearrange("p (u e) -> p u e", u=2).unsqueeze(1).to_broadcast([P, HN, 2, 2]),
+                op=ALU.mult,
+            )
+
+        def quant(codes, scales, src):
+            nc.vector.quantize_mx(out=codes.bitcast(FP8X4), scales=scales, in_=src)
+
+        def inter_p(eng, v, lo, hi):
+            dst = pg[v][:].rearrange("p (t m j) -> p t m j", t=PACK, j=PACK)[:, lo:hi]
+            src = pr[v][:].rearrange("p j (m t) -> p t m j", t=PACK)[:, lo:hi]
+            if eng == "s":
+                nc.scalar.copy(out=dst, in_=src)
+            elif eng == "g":
+                nc.gpsimd.tensor_scalar(dst, src, 1.0, 0.0, op0=ALU.mult, op1=ALU.add)
+            else:
+                nc.vector.tensor_copy(out=dst, in_=src)
+
+        def inter_w(eng, h):
+            dst = wg[h][:].rearrange("p (o j) -> p o j", j=PACK)
+            src = wr[h][:].rearrange("p j o -> p o j")
+            if eng == "g":
+                nc.gpsimd.tensor_scalar(dst, src, 1.0, 0.0, op0=ALU.mult, op1=ALU.add)
+            else:
+                nc.vector.tensor_copy(out=dst, in_=src)
+
+        def stage1(i, v, lo, hi):
+            for t in range(PACK):
+                bank = psum.tile([P, TOK], F32, name="bank")
+                cols = slice(t * P, (t + 1) * P)
+                nc.tensor.matmul_mx(
+                    out=bank[:, : hi - lo],
+                    lhsT=pc[v][:, cols].bitcast(FP8X4),
+                    lhsT_scale=psc[v][:, cols],
+                    rhs=xc[i][:, lo:hi].bitcast(FP8X4),
+                    rhs_scale=xs[i][:, lo:hi],
+                    start=True,
+                    stop=True,
+                )
+                f = v * PACK + t
+                nc.scalar.activation(
+                    out=th[i][v][:, t, lo:hi], in_=bank[:, : hi - lo], func=ACT.Tanh, bias=bh[:, f : f + 1], scale=0.5
+                )
+
+        def gain(i, h, n):
+            nc.vector.tensor_tensor(
+                out=cg[i][h][n][:].rearrange("p (n t) -> p n t", t=PACK),
+                in0=th[i][h][:, :, n * HN : (n + 1) * HN].rearrange("p t n -> p n t"),
+                in1=gh[:, h * PACK : (h + 1) * PACK].unsqueeze(1).to_broadcast([P, HN, PACK]),
+                op=ALU.mult,
+            )
+
+        def quant_c(i, h, n):
+            quant(cc[i][h][n][:], cs[i][h][n][:], cg[i][h][n][:])
+
+        pick = [(0, 0), (1, 1), (1, 0), (0, 1)]
+
+        def decode(j, r):
+            bank = psum.tile([P, OUTC], F32, name="bank")
+            n, q = divmod(r, 2)
+            cols = slice(q * P, (q + 1) * P)
+            for h in range(2):
+                i = pick[j][h]
+                nc.tensor.matmul_mx(
+                    out=bank[:],
+                    lhsT=cc[i][h][n][:, cols].bitcast(FP8X4),
+                    lhsT_scale=cs[i][h][n][:, cols],
+                    rhs=wc[h][:].bitcast(FP8X4),
+                    rhs_scale=ws[h][:],
+                    start=(h == 0),
+                    stop=(h == 1),
+                )
+            nc.vector.tensor_tensor(out=zo[j][r][:], in0=bank[:], in1=bdb[:], op=ALU.add)
+            nc.scalar.activation(out=zo[j][r][:], in_=zo[j][r][:], func=ACT.Sigmoid)
+            nc.sync.dma_start(out=out[j].rearrange("(p r) o -> p r o", r=RT)[:, r, :], in_=zo[j][r][:])
+
+        def quant_x(i, lo, hi):
+            quant(xc[i][:, lo:hi], xs[i][:, lo:hi], xg[i][:, lo * PACK : hi * PACK])
+
+        cast_x("s", 0, 0)
+        cast_x("v", 0, 1)
+        turn_x(0, 0)
+        cast_x("s", 0, 2)
+        cast_x("v", 0, 3)
+        turn_x(0, 1)
+        inter_p("s", 0, 0, 2)
+        inter_p("g", 0, 2, 4)
+        nc.vector.tensor_scalar(bh[:], b_sb[:], 0.5, None, op0=ALU.mult)
+        scale_x(0, 0)
+        quant(pc[0][:], psc[0][:], pg[0][:])
+        quant_x(0, 0, HN)
+        inter_p("g", 1, 0, 4)
+        cast_x("s", 1, 0)
+        cast_x("s", 1, 1)
+        scale_x(0, 1)
+        stage1(0, 0, 0, HN)
+        turn_x(1, 0)
+        cast_x("s", 1, 2)
+        cast_x("s", 1, 3)
+        nc.vector.tensor_scalar(gh[:], g_sb[:], 0.5, None, op0=ALU.mult)
+        quant_x(0, HN, TOK)
+        turn_x(1, 1)
+        stage1(0, 0, HN, TOK)
+        scale_x(1, 0)
+        gain(0, 0, 0)
+        quant(pc[1][:], psc[1][:], pg[1][:])
+        stage1(0, 1, 0, TOK)
+        inter_w("g", 0)
+        inter_w("g", 1)
+        scale_x(1, 1)
+        quant_c(0, 0, 0)
+        quant_x(1, 0, TOK)
+        stage1(1, 0, 0, TOK)
+        stage1(1, 1, 0, TOK)
+        gain(0, 0, 1)
+        gain(0, 1, 0)
+        quant_c(0, 0, 1)
+        gain(0, 1, 1)
+        quant_c(0, 1, 0)
+        quant(wc[0][:], ws[0][:], wg[0][:])
+        quant(wc[1][:], ws[1][:], wg[1][:])
+        quant_c(0, 1, 1)
+        decode(0, 0)
+        decode(0, 1)
+        gain(1, 0, 0)
+        decode(0, 2)
+        gain(1, 1, 0)
+        quant_c(1, 0, 0)
+        decode(0, 3)
+        quant_c(1, 1, 0)
+        decode(2, 0)
+        decode(2, 1)
+        gain(1, 0, 1)
+        decode(1, 0)
+        decode(3, 0)
+        gain(1, 1, 1)
+        quant_c(1, 0, 1)
+        decode(1, 1)
+        decode(3, 1)
+        quant_c(1, 1, 1)
+        for r in range(2, 4):
+            decode(2, r)
+            decode(1, r)
+            decode(3, r)

@@ -13,246 +13,251 @@ ACT = mybir.ActivationFunctionType
 ALU = mybir.AluOpType
 
 P = 128
+PACK = 4
 SETS = 2
+PARTS = 2
 TOK = 512
 K1 = 512
 HID = 512
 OUTC = 512
-PACK = 4
 RT = 4
-HALVES = 2
-HN = TOK // HALVES
+RUN = 4
+PSUM_BANKS = 8
+HALF = TOK // 2
 
 FLOPS = 2 * 12 * 512 * 512 * 512
+
+SCALAR, VECTOR = "scalar", "vector"
+
+PICK = [(0, 0), (1, 1), (1, 0), (0, 1)]
 
 
 def tile_switchtabmutualsalientswap_kernel(tc, x_bytes, x_scale, p, b, g, wd, bd, out):
     nc = tc.nc
     with ExitStack() as ctx:
         keep = ctx.enter_context(tc.tile_pool(name="keep", bufs=1))
-        psum = ctx.enter_context(tc.psum_pool(name="psum", bufs=8))
+        psum = ctx.enter_context(tc.psum_pool(name="psum", bufs=PSUM_BANKS))
         ctx.enter_context(tc.manual_schedule())
 
         def sb(shape, dtype, name):
             return keep.tile(shape, dtype, name=name, align_bytes=64)
 
-        xb = [sb([P, RT * K1], U8, f"xb{i}") for i in range(SETS)]
-        xw = [sb([P, RT * K1], BF16, f"xw{i}") for i in range(SETS)]
-        xg = [sb([P, TOK * PACK], BF16, f"xg{i}") for i in range(SETS)]
-        xc = [sb([P, TOK], U32, f"xc{i}") for i in range(SETS)]
-        xs = [sb([P, TOK], U8, f"xs{i}") for i in range(SETS)]
-        pr = [sb([P, PACK, HID], BF16, f"pr{v}") for v in range(2)]
-        pg = [sb([P, HID * PACK], BF16, f"pg{v}") for v in range(2)]
-        pc = [sb([P, HID], U32, f"pc{v}") for v in range(2)]
-        psc = [sb([P, HID], U8, f"psc{v}") for v in range(2)]
-        wr = [sb([P, PACK, OUTC], BF16, f"wr{h}") for h in range(2)]
-        wg = [sb([P, OUTC * PACK], BF16, f"wg{h}") for h in range(2)]
-        wc = [sb([P, OUTC], U32, f"wc{h}") for h in range(2)]
-        ws = [sb([P, OUTC], U8, f"ws{h}") for h in range(2)]
+        def grid(shape, dtype, name, *dims):
+            keys = [()]
+            for d in dims:
+                keys = [k + (i,) for k in keys for i in range(d)]
+            return {k: sb(shape, dtype, name + "_".join(str(i) for i in k)) for k in keys}
+
+        xb = grid([P, RT * K1], U8, "xb", SETS)
+        xw = grid([P, RT * K1], BF16, "xw", SETS)
+        xg = grid([P, TOK * PACK], BF16, "xg", SETS)
+        xc = grid([P, TOK], U32, "xc", SETS)
+        xs = grid([P, TOK], U8, "xs", SETS)
+        pr = grid([P, PACK, HID], BF16, "pr", PARTS)
+        pg = grid([P, HID * PACK], BF16, "pg", PARTS)
+        pc = grid([P, HID], U32, "pc", PARTS)
+        ps = grid([P, HID], U8, "ps", PARTS)
+        wr = grid([P, PACK, OUTC], BF16, "wr", PARTS)
+        wg = grid([P, OUTC * PACK], BF16, "wg", PARTS)
+        wc = grid([P, OUTC], U32, "wc", PARTS)
+        ws = grid([P, OUTC], U8, "ws", PARTS)
+        th = grid([P, PACK, TOK], F32, "th", SETS, PARTS)
+        cg = grid([P, HALF * PACK], BF16, "cg", SETS, PARTS, 2)
+        cc = grid([P, HALF], U32, "cc", SETS, PARTS, 2)
+        cs = grid([P, HALF], U8, "cs", SETS, PARTS, 2)
+        zo = grid([P, OUTC], F32, "zo", 4, RT)
         sc = sb([P, PACK], F32, "sc")
-        b_sb = sb([P, 2 * PACK], BF16, "b_sb")
-        g_sb = sb([P, 2 * PACK], BF16, "g_sb")
-        bh = sb([P, 2 * PACK], F32, "bh")
-        gh = sb([P, 2 * PACK], F32, "gh")
+        b_sb = sb([P, PARTS * PACK], BF16, "b_sb")
+        g_sb = sb([P, PARTS * PACK], BF16, "g_sb")
+        bh = sb([P, PARTS * PACK], F32, "bh")
+        gh = sb([P, PARTS * PACK], F32, "gh")
         bdb = sb([P, OUTC], BF16, "bdb")
         ident = sb([P, P], F32, "ident")
         warm = sb([P, 1], F32, "warm")
-        th = [[sb([P, PACK, TOK], F32, f"th{i}{h}") for h in range(2)] for i in range(SETS)]
-        cg = [[[sb([P, HN * PACK], BF16, f"cg{i}{h}{n}") for n in range(HALVES)] for h in range(2)] for i in range(SETS)]
-        cc = [[[sb([P, HN], U32, f"cc{i}{h}{n}") for n in range(HALVES)] for h in range(2)] for i in range(SETS)]
-        cs = [[[sb([P, HN], U8, f"cs{i}{h}{n}") for n in range(HALVES)] for h in range(2)] for i in range(SETS)]
-        zo = [[sb([P, OUTC], F32, f"zo{j}{r}") for r in range(RT)] for j in range(4)]
 
         def load_x(i, lo, hi):
-            nc.sync.dma_start(
-                out=xb[i][:, lo * K1 : hi * K1],
-                in_=x_bytes[i].rearrange("(p r) k -> p (r k)", r=RT)[:, lo * K1 : hi * K1],
-            )
+            cols = slice(lo * K1, hi * K1)
+            nc.sync.dma_start(out=xb[i,][:, cols], in_=x_bytes[i].rearrange("(q r) k -> q (r k)", r=RT)[:, cols])
 
-        def load_p(v):
-            nc.sync.dma_start(out=pr[v][:], in_=p[v].rearrange("(p j) c -> p j c", j=PACK))
+        def load_rows(tile, rows):
+            nc.sync.dma_start(out=tile[:], in_=rows.rearrange("(q s) c -> q s c", s=PACK))
+
+        def load_vector(tile, vec):
+            nc.sync.dma_start(out=tile[:].rearrange("q (v s) -> q v s", s=PACK), in_=vec)
 
         nc.gpsimd.memset(warm[:], 0.0)
         nc.scalar.activation(out=warm[:], in_=warm[:], func=ACT.Sigmoid)
         load_x(0, 0, 2)
-        load_x(0, 2, 4)
+        load_x(0, 2, RT)
+        nc.sync.dma_start(out=sc[:], in_=x_scale.rearrange("a c (q s) -> q (a c s)", s=PACK))
         make_identity(nc, ident[:])
-        load_p(0)
-        nc.sync.dma_start(out=sc[:], in_=x_scale.rearrange("a b (p t) -> p (a b t)", t=PACK))
-        nc.sync.dma_start(out=b_sb[:].rearrange("p (v t) -> p v t", t=PACK), in_=b.rearrange("v (p t) -> p v t", t=PACK))
-        load_p(1)
-        load_x(1, 0, 4)
-        nc.sync.dma_start(out=g_sb[:].rearrange("p (h t) -> p h t", t=PACK), in_=g.rearrange("(h p t) -> p h t", t=PACK, h=2))
-        for h in range(2):
-            nc.sync.dma_start(out=wr[h][:], in_=wd[h * HID : (h + 1) * HID, :].rearrange("(p j) o -> p j o", j=PACK))
+        for v in range(PARTS):
+            load_rows(pr[v,], p[v])
+        load_x(1, 0, RT)
+        load_vector(b_sb, b.rearrange("v (q s) -> q v s", s=PACK))
+        load_vector(g_sb, g.rearrange("(v q s) -> q v s", v=PARTS, s=PACK))
+        for v in range(PARTS):
+            load_rows(wr[v,], wd[v * HID : (v + 1) * HID, :])
         nc.sync.dma_start(out=bdb[:], in_=bd.partition_broadcast(P))
 
-        def cast_x(eng, i, r):
+        def widen(engine, i, r):
             cols = slice(r * K1, (r + 1) * K1)
-            if eng == "s":
-                nc.scalar.copy(out=xw[i][:, cols], in_=xb[i][:, cols].bitcast(FP8))
+            src = xb[i,][:, cols].bitcast(FP8)
+            if engine == SCALAR:
+                nc.scalar.copy(out=xw[i,][:, cols], in_=src)
             else:
-                nc.vector.tensor_copy(out=xw[i][:, cols], in_=xb[i][:, cols].bitcast(FP8))
+                nc.vector.tensor_copy(out=xw[i,][:, cols], in_=src)
 
-        xps = {}
+        turned = {}
 
-        def turn_x(i, pair):
-            words = xw[i][:].bitcast(F32)
-            bank = psum.tile([P, 2 * HN], F32, name="bank")
-            for q in range(2):
-                r = 2 * pair + q
+        def turn(i, n):
+            words = xw[i,][:].bitcast(F32)
+            bank = psum.tile([P, 2 * HALF], F32, name="bank")
+            for a in range(2):
+                first = (2 * n + a) * (K1 // 2)
                 for u in range(2):
-                    nc.tensor.transpose(
-                        bank[:, u * HN + q * P : u * HN + (q + 1) * P],
-                        words[:, r * (K1 // 2) + u : (r + 1) * (K1 // 2) : 2],
-                        ident[:],
-                    )
-            xps[i, pair] = bank
+                    lo = u * HALF + a * P
+                    nc.tensor.transpose(bank[:, lo : lo + P], words[:, first + u : first + K1 // 2 : 2], ident[:])
+            turned[i, n] = bank
 
-        def scale_x(i, pair):
+        def scale(i, n):
             nc.vector.tensor_tensor(
-                out=xg[i][:, pair * HN * PACK : (pair + 1) * HN * PACK].rearrange("p (n u e) -> p n u e", u=2, e=2),
-                in0=xps[i, pair][:].bitcast(BF16).rearrange("p (u n e) -> p n u e", u=2, e=2),
-                in1=sc[:].rearrange("p (u e) -> p u e", u=2).unsqueeze(1).to_broadcast([P, HN, 2, 2]),
+                out=xg[i,][:, n * HALF * PACK : (n + 1) * HALF * PACK].rearrange("q (m u e) -> q m u e", u=2, e=2),
+                in0=turned[i, n][:].bitcast(BF16).rearrange("q (u m e) -> q m u e", u=2, e=2),
+                in1=sc[:].rearrange("q (u e) -> q u e", u=2).unsqueeze(1).to_broadcast([P, HALF, 2, 2]),
                 op=ALU.mult,
             )
 
-        def quant(codes, scales, src):
-            nc.vector.quantize_mx(out=codes.bitcast(FP8X4), scales=scales, in_=src)
+        def quantise(codes, scales, values):
+            nc.vector.quantize_mx(out=codes[:].bitcast(FP8X4), scales=scales[:], in_=values[:])
 
-        def inter_p(eng, v, lo, hi):
-            dst = pg[v][:].rearrange("p (t m j) -> p t m j", t=PACK, j=PACK)[:, lo:hi]
-            src = pr[v][:].rearrange("p j (m t) -> p t m j", t=PACK)[:, lo:hi]
-            if eng == "s":
+        def interleave(engine, dst, src):
+            dst = dst.rearrange("q (c i s) -> q c s i", i=RUN, s=PACK)
+            src = src.rearrange("q s (c i) -> q c s i", i=RUN)
+            if engine == SCALAR:
                 nc.scalar.copy(out=dst, in_=src)
-            elif eng == "g":
-                nc.gpsimd.tensor_scalar(dst, src, 1.0, 0.0, op0=ALU.mult, op1=ALU.add)
             else:
                 nc.vector.tensor_copy(out=dst, in_=src)
 
-        def inter_w(eng, h):
-            dst = wg[h][:].rearrange("p (o j) -> p o j", j=PACK)
-            src = wr[h][:].rearrange("p j o -> p o j")
-            if eng == "g":
-                nc.gpsimd.tensor_scalar(dst, src, 1.0, 0.0, op0=ALU.mult, op1=ALU.add)
-            else:
-                nc.vector.tensor_copy(out=dst, in_=src)
+        def interleave_p(engine, v, slots):
+            for t in slots:
+                cols = slice(t * P * PACK, (t + 1) * P * PACK)
+                interleave(engine, pg[v,][:, cols], pr[v,][:].rearrange("q s (m t) -> q t s m", t=PACK)[:, t])
 
-        def stage1(i, v, lo, hi):
+        def interleave_wd(v):
+            for c in range(OUTC // P):
+                cols = slice(c * P * PACK, (c + 1) * P * PACK)
+                interleave(SCALAR, wg[v,][:, cols], wr[v,][:, :, c * P : (c + 1) * P])
+
+        def features(i, v):
             for t in range(PACK):
-                bank = psum.tile([P, TOK], F32, name="bank")
                 cols = slice(t * P, (t + 1) * P)
+                bank = psum.tile([P, TOK], F32, name="bank")
                 nc.tensor.matmul_mx(
-                    out=bank[:, : hi - lo],
-                    lhsT=pc[v][:, cols].bitcast(FP8X4),
-                    lhsT_scale=psc[v][:, cols],
-                    rhs=xc[i][:, lo:hi].bitcast(FP8X4),
-                    rhs_scale=xs[i][:, lo:hi],
+                    out=bank[:],
+                    lhsT=pc[v,][:, cols].bitcast(FP8X4),
+                    lhsT_scale=ps[v,][:, cols],
+                    rhs=xc[i,][:].bitcast(FP8X4),
+                    rhs_scale=xs[i,][:],
                     start=True,
                     stop=True,
                 )
                 f = v * PACK + t
-                nc.scalar.activation(
-                    out=th[i][v][:, t, lo:hi], in_=bank[:, : hi - lo], func=ACT.Tanh, bias=bh[:, f : f + 1], scale=0.5
-                )
+                nc.scalar.activation(out=th[i, v][:, t, :], in_=bank[:], func=ACT.Tanh, bias=bh[:, f : f + 1], scale=0.5)
 
-        def gain(i, h, n):
+        def gain(i, v, n):
             nc.vector.tensor_tensor(
-                out=cg[i][h][n][:].rearrange("p (n t) -> p n t", t=PACK),
-                in0=th[i][h][:, :, n * HN : (n + 1) * HN].rearrange("p t n -> p n t"),
-                in1=gh[:, h * PACK : (h + 1) * PACK].unsqueeze(1).to_broadcast([P, HN, PACK]),
+                out=cg[i, v, n][:].rearrange("q (c i t) -> q c t i", i=RUN, t=PACK),
+                in0=th[i, v][:, :, n * HALF : (n + 1) * HALF].rearrange("q t (c i) -> q c t i", i=RUN),
+                in1=gh[:, v * PACK : (v + 1) * PACK].unsqueeze(1).unsqueeze(3).to_broadcast([P, HALF // RUN, PACK, RUN]),
                 op=ALU.mult,
             )
 
-        def quant_c(i, h, n):
-            quant(cc[i][h][n][:], cs[i][h][n][:], cg[i][h][n][:])
+        def quantise_c(i, v, n):
+            quantise(cc[i, v, n], cs[i, v, n], cg[i, v, n])
 
-        pick = [(0, 0), (1, 1), (1, 0), (0, 1)]
-
-        def decode(j, r):
+        def decode(j, r, pieces=1):
+            n, a = divmod(r, 2)
+            cols = slice(a * P, (a + 1) * P)
             bank = psum.tile([P, OUTC], F32, name="bank")
-            n, q = divmod(r, 2)
-            cols = slice(q * P, (q + 1) * P)
-            for h in range(2):
-                i = pick[j][h]
+            for v in range(PARTS):
+                i = PICK[j][v]
                 nc.tensor.matmul_mx(
                     out=bank[:],
-                    lhsT=cc[i][h][n][:, cols].bitcast(FP8X4),
-                    lhsT_scale=cs[i][h][n][:, cols],
-                    rhs=wc[h][:].bitcast(FP8X4),
-                    rhs_scale=ws[h][:],
-                    start=(h == 0),
-                    stop=(h == 1),
+                    lhsT=cc[i, v, n][:, cols].bitcast(FP8X4),
+                    lhsT_scale=cs[i, v, n][:, cols],
+                    rhs=wc[v,][:].bitcast(FP8X4),
+                    rhs_scale=ws[v,][:],
+                    start=(v == 0),
+                    stop=(v == PARTS - 1),
                 )
-            nc.vector.tensor_tensor(out=zo[j][r][:], in0=bank[:], in1=bdb[:], op=ALU.add)
-            nc.scalar.activation(out=zo[j][r][:], in_=zo[j][r][:], func=ACT.Sigmoid)
-            nc.sync.dma_start(out=out[j].rearrange("(p r) o -> p r o", r=RT)[:, r, :], in_=zo[j][r][:])
+            for c in range(pieces):
+                oc = slice(c * OUTC // pieces, (c + 1) * OUTC // pieces)
+                z = zo[j, r][:, oc]
+                nc.vector.tensor_tensor(out=z, in0=bank[:, oc], in1=bdb[:, oc], op=ALU.add)
+                nc.scalar.activation(out=z, in_=z, func=ACT.Sigmoid)
+                nc.sync.dma_start(out=out[j].rearrange("(q r) o -> q r o", r=RT)[:, r, oc], in_=z)
 
-        def quant_x(i, lo, hi):
-            quant(xc[i][:, lo:hi], xs[i][:, lo:hi], xg[i][:, lo * PACK : hi * PACK])
+        widen(SCALAR, 0, 0)
+        widen(VECTOR, 0, 1)
+        turn(0, 0)
+        widen(SCALAR, 0, 2)
+        widen(VECTOR, 0, 3)
+        turn(0, 1)
+        interleave_p(SCALAR, 0, (0, 1))
+        scale(0, 0)
+        interleave_p(VECTOR, 0, (2, 3))
+        scale(0, 1)
+        interleave_p(SCALAR, 1, (0, 1))
+        quantise(pc[0,], ps[0,], pg[0,])
+        nc.scalar.activation(out=bh[:], in_=b_sb[:], func=ACT.Copy, scale=0.5)
+        quantise(xc[0,], xs[0,], xg[0,])
+        interleave_p(VECTOR, 1, (2, 3))
+        widen(SCALAR, 1, 0)
+        widen(SCALAR, 1, 1)
+        turn(1, 0)
+        widen(SCALAR, 1, 2)
+        widen(SCALAR, 1, 3)
+        features(0, 0)
+        turn(1, 1)
+        quantise(pc[1,], ps[1,], pg[1,])
+        nc.scalar.activation(out=gh[:], in_=g_sb[:], func=ACT.Copy, scale=0.5)
+        features(0, 1)
+        scale(1, 0)
+        scale(1, 1)
 
-        cast_x("s", 0, 0)
-        cast_x("v", 0, 1)
-        turn_x(0, 0)
-        cast_x("s", 0, 2)
-        cast_x("v", 0, 3)
-        turn_x(0, 1)
-        inter_p("s", 0, 0, 2)
-        inter_p("g", 0, 2, 4)
-        nc.vector.tensor_scalar(bh[:], b_sb[:], 0.5, None, op0=ALU.mult)
-        scale_x(0, 0)
-        quant(pc[0][:], psc[0][:], pg[0][:])
-        quant_x(0, 0, HN)
-        inter_p("g", 1, 0, 4)
-        cast_x("s", 1, 0)
-        cast_x("s", 1, 1)
-        scale_x(0, 1)
-        stage1(0, 0, 0, HN)
-        turn_x(1, 0)
-        cast_x("s", 1, 2)
-        cast_x("s", 1, 3)
-        nc.vector.tensor_scalar(gh[:], g_sb[:], 0.5, None, op0=ALU.mult)
-        quant_x(0, HN, TOK)
-        turn_x(1, 1)
-        stage1(0, 0, HN, TOK)
-        scale_x(1, 0)
         gain(0, 0, 0)
-        quant(pc[1][:], psc[1][:], pg[1][:])
-        stage1(0, 1, 0, TOK)
-        inter_w("g", 0)
-        inter_w("g", 1)
-        scale_x(1, 1)
-        quant_c(0, 0, 0)
-        quant_x(1, 0, TOK)
-        stage1(1, 0, 0, TOK)
-        stage1(1, 1, 0, TOK)
         gain(0, 0, 1)
+        quantise(xc[1,], xs[1,], xg[1,])
+        quantise_c(0, 0, 0)
         gain(0, 1, 0)
-        quant_c(0, 0, 1)
+        quantise_c(0, 0, 1)
+        interleave_wd(0)
+        features(1, 0)
         gain(0, 1, 1)
-        quant_c(0, 1, 0)
-        quant(wc[0][:], ws[0][:], wg[0][:])
-        quant(wc[1][:], ws[1][:], wg[1][:])
-        quant_c(0, 1, 1)
+        quantise_c(0, 1, 0)
+        quantise(wc[0,], ws[0,], wg[0,])
+        quantise_c(0, 1, 1)
+        interleave_wd(1)
+        gain(1, 0, 0)
+        gain(1, 0, 1)
+        quantise_c(1, 0, 0)
+        quantise(wc[1,], ws[1,], wg[1,])
+        quantise_c(1, 0, 1)
+        features(1, 1)
+
         decode(0, 0)
         decode(0, 1)
-        gain(1, 0, 0)
-        decode(0, 2)
-        gain(1, 1, 0)
-        quant_c(1, 0, 0)
-        decode(0, 3)
-        quant_c(1, 1, 0)
         decode(2, 0)
         decode(2, 1)
-        gain(1, 0, 1)
-        decode(1, 0)
-        decode(3, 0)
+        gain(1, 1, 0)
+        decode(0, 2)
+        decode(0, 3)
         gain(1, 1, 1)
-        quant_c(1, 0, 1)
-        decode(1, 1)
-        decode(3, 1)
-        quant_c(1, 1, 1)
-        for r in range(2, 4):
-            decode(2, r)
+        quantise_c(1, 1, 0)
+        decode(2, 2)
+        decode(2, 3)
+        quantise_c(1, 1, 1)
+        for r in range(RT):
             decode(1, r)
-            decode(3, r)
+            decode(3, r, pieces=2 if r == RT - 1 else 1)

from contextlib import ExitStack

import concourse.mybir as mybir
from concourse.masks import make_identity

F32 = mybir.dt.float32
BF16 = mybir.dt.bfloat16
U32 = mybir.dt.uint32
U8 = mybir.dt.uint8
FP8 = mybir.dt.float8_e4m3fn
FP8X4 = mybir.dt.float8_e4m3fn_x4
ACT = mybir.ActivationFunctionType
ALU = mybir.AluOpType

P = 128
PACK = 4
SETS = 2
PARTS = 2
TOK = 512
K1 = 512
HID = 512
OUTC = 512
RT = 4
RUN = 4
PSUM_BANKS = 8
HALF = TOK // 2

FLOPS = 2 * 12 * 512 * 512 * 512

SCALAR, VECTOR = "scalar", "vector"

PICK = [(0, 0), (1, 1), (1, 0), (0, 1)]


def tile_switchtabmutualsalientswap_kernel(tc, x_bytes, x_scale, p, b, g, wd, bd, out):
    nc = tc.nc
    with ExitStack() as ctx:
        keep = ctx.enter_context(tc.tile_pool(name="keep", bufs=1))
        psum = ctx.enter_context(tc.psum_pool(name="psum", bufs=PSUM_BANKS))
        ctx.enter_context(tc.manual_schedule())

        def sb(shape, dtype, name):
            return keep.tile(shape, dtype, name=name, align_bytes=64)

        def grid(shape, dtype, name, *dims):
            keys = [()]
            for d in dims:
                keys = [k + (i,) for k in keys for i in range(d)]
            return {k: sb(shape, dtype, name + "_".join(str(i) for i in k)) for k in keys}

        xb = grid([P, RT * K1], U8, "xb", SETS)
        xw = grid([P, RT * K1], BF16, "xw", SETS)
        xg = grid([P, TOK * PACK], BF16, "xg", SETS)
        xc = grid([P, TOK], U32, "xc", SETS)
        xs = grid([P, TOK], U8, "xs", SETS)
        pr = grid([P, PACK, HID], BF16, "pr", PARTS)
        pg = grid([P, HID * PACK], BF16, "pg", PARTS)
        pc = grid([P, HID], U32, "pc", PARTS)
        ps = grid([P, HID], U8, "ps", PARTS)
        wr = grid([P, PACK, OUTC], BF16, "wr", PARTS)
        wg = grid([P, OUTC * PACK], BF16, "wg", PARTS)
        wc = grid([P, OUTC], U32, "wc", PARTS)
        ws = grid([P, OUTC], U8, "ws", PARTS)
        th = grid([P, PACK, TOK], F32, "th", SETS, PARTS)
        cg = grid([P, HALF * PACK], BF16, "cg", SETS, PARTS, 2)
        cc = grid([P, HALF], U32, "cc", SETS, PARTS, 2)
        cs = grid([P, HALF], U8, "cs", SETS, PARTS, 2)
        zo = grid([P, OUTC], F32, "zo", 4, RT)
        sc = sb([P, PACK], F32, "sc")
        b_sb = sb([P, PARTS * PACK], BF16, "b_sb")
        g_sb = sb([P, PARTS * PACK], BF16, "g_sb")
        bh = sb([P, PARTS * PACK], F32, "bh")
        gh = sb([P, PARTS * PACK], F32, "gh")
        bdb = sb([P, OUTC], BF16, "bdb")
        ident = sb([P, P], F32, "ident")
        warm = sb([P, 1], F32, "warm")

        def load_x(i, lo, hi):
            cols = slice(lo * K1, hi * K1)
            nc.sync.dma_start(out=xb[i,][:, cols], in_=x_bytes[i].rearrange("(q r) k -> q (r k)", r=RT)[:, cols])

        def load_rows(tile, rows):
            nc.sync.dma_start(out=tile[:], in_=rows.rearrange("(q s) c -> q s c", s=PACK))

        def load_vector(tile, vec):
            nc.sync.dma_start(out=tile[:].rearrange("q (v s) -> q v s", s=PACK), in_=vec)

        nc.gpsimd.memset(warm[:], 0.0)
        nc.scalar.activation(out=warm[:], in_=warm[:], func=ACT.Sigmoid)
        load_x(0, 0, 2)
        load_x(0, 2, RT)
        nc.sync.dma_start(out=sc[:], in_=x_scale.rearrange("a c (q s) -> q (a c s)", s=PACK))
        make_identity(nc, ident[:])
        for v in range(PARTS):
            load_rows(pr[v,], p[v])
        load_x(1, 0, RT)
        load_vector(b_sb, b.rearrange("v (q s) -> q v s", s=PACK))
        load_vector(g_sb, g.rearrange("(v q s) -> q v s", v=PARTS, s=PACK))
        for v in range(PARTS):
            load_rows(wr[v,], wd[v * HID : (v + 1) * HID, :])
        nc.sync.dma_start(out=bdb[:], in_=bd.partition_broadcast(P))

        def widen(engine, i, r):
            cols = slice(r * K1, (r + 1) * K1)
            src = xb[i,][:, cols].bitcast(FP8)
            if engine == SCALAR:
                nc.scalar.copy(out=xw[i,][:, cols], in_=src)
            else:
                nc.vector.tensor_copy(out=xw[i,][:, cols], in_=src)

        turned = {}

        def turn(i, n):
            words = xw[i,][:].bitcast(F32)
            bank = psum.tile([P, 2 * HALF], F32, name="bank")
            for a in range(2):
                first = (2 * n + a) * (K1 // 2)
                for u in range(2):
                    lo = u * HALF + a * P
                    nc.tensor.transpose(bank[:, lo : lo + P], words[:, first + u : first + K1 // 2 : 2], ident[:])
            turned[i, n] = bank

        def scale(i, n):
            nc.vector.tensor_tensor(
                out=xg[i,][:, n * HALF * PACK : (n + 1) * HALF * PACK].rearrange("q (m u e) -> q m u e", u=2, e=2),
                in0=turned[i, n][:].bitcast(BF16).rearrange("q (u m e) -> q m u e", u=2, e=2),
                in1=sc[:].rearrange("q (u e) -> q u e", u=2).unsqueeze(1).to_broadcast([P, HALF, 2, 2]),
                op=ALU.mult,
            )

        def quantise(codes, scales, values):
            nc.vector.quantize_mx(out=codes[:].bitcast(FP8X4), scales=scales[:], in_=values[:])

        def interleave(engine, dst, src):
            dst = dst.rearrange("q (c i s) -> q c s i", i=RUN, s=PACK)
            src = src.rearrange("q s (c i) -> q c s i", i=RUN)
            if engine == SCALAR:
                nc.scalar.copy(out=dst, in_=src)
            else:
                nc.vector.tensor_copy(out=dst, in_=src)

        def interleave_p(engine, v, slots):
            for t in slots:
                cols = slice(t * P * PACK, (t + 1) * P * PACK)
                interleave(engine, pg[v,][:, cols], pr[v,][:].rearrange("q s (m t) -> q t s m", t=PACK)[:, t])

        def interleave_wd(v):
            for c in range(OUTC // P):
                cols = slice(c * P * PACK, (c + 1) * P * PACK)
                interleave(SCALAR, wg[v,][:, cols], wr[v,][:, :, c * P : (c + 1) * P])

        def features(i, v):
            for t in range(PACK):
                cols = slice(t * P, (t + 1) * P)
                bank = psum.tile([P, TOK], F32, name="bank")
                nc.tensor.matmul_mx(
                    out=bank[:],
                    lhsT=pc[v,][:, cols].bitcast(FP8X4),
                    lhsT_scale=ps[v,][:, cols],
                    rhs=xc[i,][:].bitcast(FP8X4),
                    rhs_scale=xs[i,][:],
                    start=True,
                    stop=True,
                )
                f = v * PACK + t
                nc.scalar.activation(out=th[i, v][:, t, :], in_=bank[:], func=ACT.Tanh, bias=bh[:, f : f + 1], scale=0.5)

        def gain(i, v, n):
            nc.vector.tensor_tensor(
                out=cg[i, v, n][:].rearrange("q (c i t) -> q c t i", i=RUN, t=PACK),
                in0=th[i, v][:, :, n * HALF : (n + 1) * HALF].rearrange("q t (c i) -> q c t i", i=RUN),
                in1=gh[:, v * PACK : (v + 1) * PACK].unsqueeze(1).unsqueeze(3).to_broadcast([P, HALF // RUN, PACK, RUN]),
                op=ALU.mult,
            )

        def quantise_c(i, v, n):
            quantise(cc[i, v, n], cs[i, v, n], cg[i, v, n])

        def decode(j, r, pieces=1):
            n, a = divmod(r, 2)
            cols = slice(a * P, (a + 1) * P)
            bank = psum.tile([P, OUTC], F32, name="bank")
            for v in range(PARTS):
                i = PICK[j][v]
                nc.tensor.matmul_mx(
                    out=bank[:],
                    lhsT=cc[i, v, n][:, cols].bitcast(FP8X4),
                    lhsT_scale=cs[i, v, n][:, cols],
                    rhs=wc[v,][:].bitcast(FP8X4),
                    rhs_scale=ws[v,][:],
                    start=(v == 0),
                    stop=(v == PARTS - 1),
                )
            for c in range(pieces):
                oc = slice(c * OUTC // pieces, (c + 1) * OUTC // pieces)
                z = zo[j, r][:, oc]
                nc.vector.tensor_tensor(out=z, in0=bank[:, oc], in1=bdb[:, oc], op=ALU.add)
                nc.scalar.activation(out=z, in_=z, func=ACT.Sigmoid)
                nc.sync.dma_start(out=out[j].rearrange("(q r) o -> q r o", r=RT)[:, r, oc], in_=z)

        widen(SCALAR, 0, 0)
        widen(VECTOR, 0, 1)
        turn(0, 0)
        widen(SCALAR, 0, 2)
        widen(VECTOR, 0, 3)
        turn(0, 1)
        interleave_p(SCALAR, 0, (0, 1))
        scale(0, 0)
        interleave_p(VECTOR, 0, (2, 3))
        scale(0, 1)
        interleave_p(SCALAR, 1, (0, 1))
        quantise(pc[0,], ps[0,], pg[0,])
        nc.scalar.activation(out=bh[:], in_=b_sb[:], func=ACT.Copy, scale=0.5)
        quantise(xc[0,], xs[0,], xg[0,])
        interleave_p(VECTOR, 1, (2, 3))
        widen(SCALAR, 1, 0)
        widen(SCALAR, 1, 1)
        turn(1, 0)
        widen(SCALAR, 1, 2)
        widen(SCALAR, 1, 3)
        features(0, 0)
        turn(1, 1)
        quantise(pc[1,], ps[1,], pg[1,])
        nc.scalar.activation(out=gh[:], in_=g_sb[:], func=ACT.Copy, scale=0.5)
        features(0, 1)
        scale(1, 0)
        scale(1, 1)

        gain(0, 0, 0)
        gain(0, 0, 1)
        quantise(xc[1,], xs[1,], xg[1,])
        quantise_c(0, 0, 0)
        gain(0, 1, 0)
        quantise_c(0, 0, 1)
        interleave_wd(0)
        features(1, 0)
        gain(0, 1, 1)
        quantise_c(0, 1, 0)
        quantise(wc[0,], ws[0,], wg[0,])
        quantise_c(0, 1, 1)
        interleave_wd(1)
        gain(1, 0, 0)
        gain(1, 0, 1)
        quantise_c(1, 0, 0)
        quantise(wc[1,], ws[1,], wg[1,])
        quantise_c(1, 0, 1)
        features(1, 1)

        decode(0, 0)
        decode(0, 1)
        decode(2, 0)
        decode(2, 1)
        gain(1, 1, 0)
        decode(0, 2)
        decode(0, 3)
        gain(1, 1, 1)
        quantise_c(1, 1, 0)
        decode(2, 2)
        decode(2, 3)
        quantise_c(1, 1, 1)
        for r in range(RT):
            decode(1, r)
            decode(3, r, pieces=2 if r == RT - 1 else 1)
